import numpy as np
CORES = [32,40,160,168]
N = 4
def setup_inputs(rng):
    return {"x": rng.standard_normal((N, 128, 2048), dtype=np.float32)}
def reference(x):
    s = x.sum(axis=0, dtype=np.float64).astype(x.dtype)
    p = 128 // N
    return {"y": np.stack([s[r * p:(r + 1) * p, :] for r in range(N)])}

@@ -1,0 +1,86 @@
+from concourse.bass import DstId, RemoteDMATransfer
+from concourse.mybir import AluOpType
+W = 512
+NP = 1
+FOLD = (2, 6)
+RELAY = (4, 5)
+WP = W // NP
+RP = 32 // NP
+SCRATCH = {'st': ('sbuf', [128, 3 * W], 'float32'), 'in0': ('sbuf', [128, W], 'float32'), 'in1': ('sbuf', [128, W], 'float32')}
+SEMAPHORES = ['y0', 'sent'] + [n + str(j) for j in range(4) for n in ('ldd', 'lds', 'ldm', 'gota', 'gotb', 'acca', 'accb')]
+
+def masks(lo, n, parts):
+    e = n // parts
+    return [(1 << e) - 1 << lo + i * e for i in range(parts)]
+
+def rank_program(g, core, T, topo):
+    k = core % 8
+    r = T.rank_of(core - k)
+    if r is None:
+        return
+    home, mate, peer = (T.cores[r], T.cores[r ^ 1], T.cores[r ^ 2])
+    S = T.sem
+    ldd = [S.ldd0, S.ldd1, S.ldd2, S.ldd3]
+    lds = [S.lds0, S.lds1, S.lds2, S.lds3]
+    ldm = [S.ldm0, S.ldm1, S.ldm2, S.ldm3]
+    gota = [S.gota0, S.gota1, S.gota2, S.gota3]
+    gotb = [S.gotb0, S.gotb1, S.gotb2, S.gotb3]
+    acca = [S.acca0, S.acca1, S.acca2, S.acca3]
+    accb = [S.accb0, S.accb1, S.accb2, S.accb3]
+
+    def tr(dst, srcs, out, mask, rsem):
+        rid, pid = topo.addr(dst, core)
+        return RemoteDMATransfer(dst_ids=[DstId(rid=rid, pnc=pid)], dma_engine_mask=mask, remote_sem=rsem, srcs=srcs, dsts=[out], alu_op=1 if len(srcs) > 1 else 0)
+    nf, nr = (len(FOLD), len(RELAY))
+    wf = WP // nf
+    if k == 0:
+        sent = 0
+        for j in range(NP):
+            for b, (t, ld) in enumerate(((r ^ 3, ldd), (r ^ 2, lds), (r ^ 1, ldm))):
+                g.dma_start(out=T.st[:, b * W + j * WP:b * W + (j + 1) * WP], in_=T.x[32 * t + j * RP:32 * t + (j + 1) * RP, :]).then_inc(ld[j], 16)
+        for j in range(NP):
+            c0 = j * WP
+            g.wait_ge(ldd[j], 16)
+            ms = masks(0, 8, nf)
+            g.remote_dma_fused([tr(peer + f, [T.st[:, c0 + i * wf:c0 + (i + 1) * wf]], T.in1[:, c0 + i * wf:c0 + (i + 1) * wf], ms[i], gotb[j]) for i, f in enumerate(FOLD)], local_sem=S.sent)
+            sent += 8
+            g.wait_ge(lds[j], 16)
+            if nr:
+                wr = WP // nr
+                ms = masks(8, 8, nr)
+                g.remote_dma_fused([tr(home + f, [T.st[:, W + c0 + i * wr:W + c0 + (i + 1) * wr]], T.in0[:, c0 + i * wr:c0 + (i + 1) * wr], ms[i], gota[j]) for i, f in enumerate(RELAY)], local_sem=S.sent)
+            else:
+                g.remote_dma_fused([tr(peer, [T.st[:, W + c0:W + c0 + WP]], T.in0[:, c0:c0 + WP], 255, gota[j])], local_sem=S.sent)
+            sent += 8
+            g.wait_ge(ldm[j], 16)
+            ms = masks(8, 8, nf)
+            g.remote_dma_fused([tr(home + f, [T.st[:, 2 * W + c0 + i * wf:2 * W + c0 + (i + 1) * wf]], T.in0[:, c0 + i * wf:c0 + (i + 1) * wf], ms[i], gota[j]) for i, f in enumerate(FOLD)], local_sem=S.sent)
+            sent += 8
+        g.dma_start(out=T.y[:, :], in_=T.x[32 * r:32 * r + 32, :]).then_inc(S.y0, 16)
+        g.wait_ge(S.y0, 16)
+        for j in range(NP):
+            g.wait_ge(gota[j], 8 * max(nr, 1))
+            g.dma_start(out=T.y[j * RP:(j + 1) * RP, :], in_=T.in0[:, j * WP:(j + 1) * WP], accum_op=AluOpType.add).then_inc(acca[j], 16)
+        for j in range(NP):
+            g.wait_ge(acca[j], 16)
+            g.wait_ge(gotb[j], 8 * nf)
+            g.dma_start(out=T.y[j * RP:(j + 1) * RP, :], in_=T.in1[:, j * WP:(j + 1) * WP], accum_op=AluOpType.add).then_inc(accb[j], 16)
+        for j in range(NP):
+            g.wait_ge(accb[j], 16)
+        g.wait_ge(S.sent, sent)
+    elif k in FOLD:
+        i = FOLD.index(k)
+        for j in range(NP):
+            c = slice(j * WP + i * wf, j * WP + (i + 1) * wf)
+            g.wait_ge(gota[j], 8 // nf)
+            g.wait_ge(gotb[j], 8 // nf)
+            g.remote_dma_fused([tr(mate, [T.in0[:, c], T.in1[:, c]], T.in1[:, c], 255, gotb[j])], local_sem=S.sent)
+        g.wait_ge(S.sent, 8 * NP)
+    elif k in RELAY:
+        i = RELAY.index(k)
+        wr = WP // nr
+        for j in range(NP):
+            c = slice(j * WP + i * wr, j * WP + (i + 1) * wr)
+            g.wait_ge(gota[j], 8 // nr)
+            g.remote_dma_fused([tr(peer, [T.in0[:, c]], T.in0[:, c], 255, gota[j])], local_sem=S.sent)
+        g.wait_ge(S.sent, 8 * NP)

@@ -1,17 +1,14 @@
 from concourse.bass import DstId, RemoteDMATransfer
 from concourse.mybir import AluOpType
+
 W = 512
-NP = 1
 FOLD = (2, 6)
 RELAY = (4, 5)
-WP = W // NP
-RP = 32 // NP
-SCRATCH = {'st': ('sbuf', [128, 3 * W], 'float32'), 'in0': ('sbuf', [128, W], 'float32'), 'in1': ('sbuf', [128, W], 'float32')}
-SEMAPHORES = ['y0', 'sent'] + [n + str(j) for j in range(4) for n in ('ldd', 'lds', 'ldm', 'gota', 'gotb', 'acca', 'accb')]
+SCRATCH = {'st': ('sbuf', [128, 3 * W], 'float32'),
+           'in0': ('sbuf', [128, W], 'float32'),
+           'in1': ('sbuf', [128, W], 'float32')}
+SEMAPHORES = ['y0', 'sent', 'ldd', 'lds', 'ldm', 'gota', 'gotb', 'acca', 'accb']
 
-def masks(lo, n, parts):
-    e = n // parts
-    return [(1 << e) - 1 << lo + i * e for i in range(parts)]
 
 def rank_program(g, core, T, topo):
     k = core % 8
@@ -20,67 +17,47 @@ def rank_program(g, core, T, topo):
         return
     home, mate, peer = (T.cores[r], T.cores[r ^ 1], T.cores[r ^ 2])
     S = T.sem
-    ldd = [S.ldd0, S.ldd1, S.ldd2, S.ldd3]
-    lds = [S.lds0, S.lds1, S.lds2, S.lds3]
-    ldm = [S.ldm0, S.ldm1, S.ldm2, S.ldm3]
-    gota = [S.gota0, S.gota1, S.gota2, S.gota3]
-    gotb = [S.gotb0, S.gotb1, S.gotb2, S.gotb3]
-    acca = [S.acca0, S.acca1, S.acca2, S.acca3]
-    accb = [S.accb0, S.accb1, S.accb2, S.accb3]
 
     def tr(dst, srcs, out, mask, rsem):
         rid, pid = topo.addr(dst, core)
-        return RemoteDMATransfer(dst_ids=[DstId(rid=rid, pnc=pid)], dma_engine_mask=mask, remote_sem=rsem, srcs=srcs, dsts=[out], alu_op=1 if len(srcs) > 1 else 0)
-    nf, nr = (len(FOLD), len(RELAY))
-    wf = WP // nf
+        return RemoteDMATransfer(dst_ids=[DstId(rid=rid, pnc=pid)], dma_engine_mask=mask, remote_sem=rsem,
+                                 srcs=srcs, dsts=[out], alu_op=1 if len(srcs) > 1 else 0)
+
+    H = W // 2
     if k == 0:
-        sent = 0
-        for j in range(NP):
-            for b, (t, ld) in enumerate(((r ^ 3, ldd), (r ^ 2, lds), (r ^ 1, ldm))):
-                g.dma_start(out=T.st[:, b * W + j * WP:b * W + (j + 1) * WP], in_=T.x[32 * t + j * RP:32 * t + (j + 1) * RP, :]).then_inc(ld[j], 16)
-        for j in range(NP):
-            c0 = j * WP
-            g.wait_ge(ldd[j], 16)
-            ms = masks(0, 8, nf)
-            g.remote_dma_fused([tr(peer + f, [T.st[:, c0 + i * wf:c0 + (i + 1) * wf]], T.in1[:, c0 + i * wf:c0 + (i + 1) * wf], ms[i], gotb[j]) for i, f in enumerate(FOLD)], local_sem=S.sent)
-            sent += 8
-            g.wait_ge(lds[j], 16)
-            if nr:
-                wr = WP // nr
-                ms = masks(8, 8, nr)
-                g.remote_dma_fused([tr(home + f, [T.st[:, W + c0 + i * wr:W + c0 + (i + 1) * wr]], T.in0[:, c0 + i * wr:c0 + (i + 1) * wr], ms[i], gota[j]) for i, f in enumerate(RELAY)], local_sem=S.sent)
-            else:
-                g.remote_dma_fused([tr(peer, [T.st[:, W + c0:W + c0 + WP]], T.in0[:, c0:c0 + WP], 255, gota[j])], local_sem=S.sent)
-            sent += 8
-            g.wait_ge(ldm[j], 16)
-            ms = masks(8, 8, nf)
-            g.remote_dma_fused([tr(home + f, [T.st[:, 2 * W + c0 + i * wf:2 * W + c0 + (i + 1) * wf]], T.in0[:, c0 + i * wf:c0 + (i + 1) * wf], ms[i], gota[j]) for i, f in enumerate(FOLD)], local_sem=S.sent)
-            sent += 8
-        g.dma_start(out=T.y[:, :], in_=T.x[32 * r:32 * r + 32, :]).then_inc(S.y0, 16)
+        def blk(t):
+            return T.x[32 * t:32 * t + 32, :]
+        g.sync.dma_start(T.st[:, 0:W], blk(r ^ 3)).then_inc(S.ldd, 16)
+        g.scalar.dma_start(T.st[:, W:2 * W], blk(r ^ 2)).then_inc(S.lds, 16)
+        g.sync.dma_start(T.st[:, 2 * W:3 * W], blk(r ^ 1)).then_inc(S.ldm, 16)
+        g.scalar.dma_start(T.y[:, :], blk(r)).then_inc(S.y0, 16)
+        g.wait_ge(S.ldd, 16)
+        g.remote_dma_fused([tr(peer + f, [T.st[:, i * H:(i + 1) * H]], T.in1[:, i * H:(i + 1) * H], 15 << 4 * i, S.gotb)
+                            for i, f in enumerate(FOLD)], local_sem=S.sent)
+        g.wait_ge(S.lds, 16)
+        g.remote_dma_fused([tr(home + f, [T.st[:, W + i * H:W + (i + 1) * H]], T.in0[:, i * H:(i + 1) * H], 15 << 8 + 4 * i, S.gota)
+                            for i, f in enumerate(RELAY)], local_sem=S.sent)
+        g.wait_ge(S.ldm, 16)
+        g.remote_dma_fused([tr(home + f, [T.st[:, 2 * W + i * H:2 * W + (i + 1) * H]], T.in0[:, i * H:(i + 1) * H], 15 << 8 + 4 * i, S.gota)
+                            for i, f in enumerate(FOLD)], local_sem=S.sent)
         g.wait_ge(S.y0, 16)
-        for j in range(NP):
-            g.wait_ge(gota[j], 8 * max(nr, 1))
-            g.dma_start(out=T.y[j * RP:(j + 1) * RP, :], in_=T.in0[:, j * WP:(j + 1) * WP], accum_op=AluOpType.add).then_inc(acca[j], 16)
-        for j in range(NP):
-            g.wait_ge(acca[j], 16)
-            g.wait_ge(gotb[j], 8 * nf)
-            g.dma_start(out=T.y[j * RP:(j + 1) * RP, :], in_=T.in1[:, j * WP:(j + 1) * WP], accum_op=AluOpType.add).then_inc(accb[j], 16)
-        for j in range(NP):
-            g.wait_ge(accb[j], 16)
-        g.wait_ge(S.sent, sent)
+        g.wait_ge(S.gota, 16)
+        g.dma_start(out=T.y[:, :], in_=T.in0[:, :], accum_op=AluOpType.add).then_inc(S.acca, 16)
+        g.wait_ge(S.acca, 16)
+        g.wait_ge(S.gotb, 16)
+        g.dma_start(out=T.y[:, :], in_=T.in1[:, :], accum_op=AluOpType.add).then_inc(S.accb, 16)
+        g.wait_ge(S.accb, 16)
+        g.wait_ge(S.sent, 24)
     elif k in FOLD:
         i = FOLD.index(k)
-        for j in range(NP):
-            c = slice(j * WP + i * wf, j * WP + (i + 1) * wf)
-            g.wait_ge(gota[j], 8 // nf)
-            g.wait_ge(gotb[j], 8 // nf)
-            g.remote_dma_fused([tr(mate, [T.in0[:, c], T.in1[:, c]], T.in1[:, c], 255, gotb[j])], local_sem=S.sent)
-        g.wait_ge(S.sent, 8 * NP)
+        c = slice(i * H, (i + 1) * H)
+        g.wait_ge(S.gota, 4)
+        g.wait_ge(S.gotb, 4)
+        g.remote_dma_fused([tr(mate, [T.in0[:, c], T.in1[:, c]], T.in1[:, c], 255, S.gotb)], local_sem=S.sent)
+        g.wait_ge(S.sent, 8)
     elif k in RELAY:
         i = RELAY.index(k)
-        wr = WP // nr
-        for j in range(NP):
-            c = slice(j * WP + i * wr, j * WP + (i + 1) * wr)
-            g.wait_ge(gota[j], 8 // nr)
-            g.remote_dma_fused([tr(peer, [T.in0[:, c]], T.in0[:, c], 255, gota[j])], local_sem=S.sent)
-        g.wait_ge(S.sent, 8 * NP)
+        c = slice(i * H, (i + 1) * H)
+        g.wait_ge(S.gota, 4)
+        g.remote_dma_fused([tr(peer, [T.in0[:, c]], T.in0[:, c], 255, S.gota)], local_sem=S.sent)
+        g.wait_ge(S.sent, 8)

@@ -4,9 +4,9 @@ from concourse.mybir import AluOpType
 W = 512
 FOLD = (2, 6)
 RELAY = (4, 5)
-SCRATCH = {'st': ('sbuf', [128, 3 * W], 'float32'),
-           'in0': ('sbuf', [128, W], 'float32'),
-           'in1': ('sbuf', [128, W], 'float32')}
+SCRATCH = {'st': ('dram', [6, 128, W // 2], 'float32'),
+           'in0': ('dram', [2, 128, W // 2], 'float32'),
+           'in1': ('dram', [2, 128, W // 2], 'float32')}
 SEMAPHORES = ['y0', 'sent', 'ldd', 'lds', 'ldm', 'gota', 'gotb', 'acca', 'accb']
 
 
@@ -23,41 +23,38 @@ def rank_program(g, core, T, topo):
         return RemoteDMATransfer(dst_ids=[DstId(rid=rid, pnc=pid)], dma_engine_mask=mask, remote_sem=rsem,
                                  srcs=srcs, dsts=[out], alu_op=1 if len(srcs) > 1 else 0)
 
-    H = W // 2
     if k == 0:
         def blk(t):
             return T.x[32 * t:32 * t + 32, :]
-        g.sync.dma_start(T.st[:, 0:W], blk(r ^ 3)).then_inc(S.ldd, 16)
-        g.scalar.dma_start(T.st[:, W:2 * W], blk(r ^ 2)).then_inc(S.lds, 16)
-        g.sync.dma_start(T.st[:, 2 * W:3 * W], blk(r ^ 1)).then_inc(S.ldm, 16)
+        g.sync.dma_start(T.st[0:2], blk(r ^ 3)).then_inc(S.ldd, 16)
+        g.scalar.dma_start(T.st[2:4], blk(r ^ 2)).then_inc(S.lds, 16)
+        g.sync.dma_start(T.st[4:6], blk(r ^ 1)).then_inc(S.ldm, 16)
         g.scalar.dma_start(T.y[:, :], blk(r)).then_inc(S.y0, 16)
         g.wait_ge(S.ldd, 16)
-        g.remote_dma_fused([tr(peer + f, [T.st[:, i * H:(i + 1) * H]], T.in1[:, i * H:(i + 1) * H], 15 << 4 * i, S.gotb)
+        g.remote_dma_fused([tr(peer + f, [T.st[i]], T.in1[i], 15 << 4 * i, S.gotb)
                             for i, f in enumerate(FOLD)], local_sem=S.sent)
         g.wait_ge(S.lds, 16)
-        g.remote_dma_fused([tr(home + f, [T.st[:, W + i * H:W + (i + 1) * H]], T.in0[:, i * H:(i + 1) * H], 15 << 8 + 4 * i, S.gota)
+        g.remote_dma_fused([tr(home + f, [T.st[2 + i]], T.in0[i], 15 << 8 + 4 * i, S.gota)
                             for i, f in enumerate(RELAY)], local_sem=S.sent)
         g.wait_ge(S.ldm, 16)
-        g.remote_dma_fused([tr(home + f, [T.st[:, 2 * W + i * H:2 * W + (i + 1) * H]], T.in0[:, i * H:(i + 1) * H], 15 << 8 + 4 * i, S.gota)
+        g.remote_dma_fused([tr(home + f, [T.st[4 + i]], T.in0[i], 15 << 8 + 4 * i, S.gota)
                             for i, f in enumerate(FOLD)], local_sem=S.sent)
         g.wait_ge(S.y0, 16)
         g.wait_ge(S.gota, 16)
-        g.dma_start(out=T.y[:, :], in_=T.in0[:, :], accum_op=AluOpType.add).then_inc(S.acca, 16)
+        g.dma_start(out=T.y[:, :], in_=T.in0[:], accum_op=AluOpType.add, max_dma_last_dim=8192).then_inc(S.acca, 16)
         g.wait_ge(S.acca, 16)
         g.wait_ge(S.gotb, 16)
-        g.dma_start(out=T.y[:, :], in_=T.in1[:, :], accum_op=AluOpType.add).then_inc(S.accb, 16)
+        g.dma_start(out=T.y[:, :], in_=T.in1[:], accum_op=AluOpType.add, max_dma_last_dim=8192).then_inc(S.accb, 16)
         g.wait_ge(S.accb, 16)
         g.wait_ge(S.sent, 24)
     elif k in FOLD:
         i = FOLD.index(k)
-        c = slice(i * H, (i + 1) * H)
         g.wait_ge(S.gota, 4)
         g.wait_ge(S.gotb, 4)
-        g.remote_dma_fused([tr(mate, [T.in0[:, c], T.in1[:, c]], T.in1[:, c], 255, S.gotb)], local_sem=S.sent)
+        g.remote_dma_fused([tr(mate, [T.in0[i], T.in1[i]], T.in1[i], 255, S.gotb)], local_sem=S.sent)
         g.wait_ge(S.sent, 8)
     elif k in RELAY:
         i = RELAY.index(k)
-        c = slice(i * H, (i + 1) * H)
         g.wait_ge(S.gota, 4)
-        g.remote_dma_fused([tr(peer, [T.in0[:, c]], T.in0[:, c], 255, S.gota)], local_sem=S.sent)
+        g.remote_dma_fused([tr(peer, [T.in0[i]], T.in0[i], 255, S.gota)], local_sem=S.sent)
         g.wait_ge(S.sent, 8)

@@ -1,13 +1,11 @@
 from concourse.bass import DstId, RemoteDMATransfer
 from concourse.mybir import AluOpType
 
-W = 512
-FOLD = (2, 6)
-RELAY = (4, 5)
-SCRATCH = {'st': ('dram', [6, 128, W // 2], 'float32'),
-           'in0': ('dram', [2, 128, W // 2], 'float32'),
-           'in1': ('dram', [2, 128, W // 2], 'float32')}
-SEMAPHORES = ['y0', 'sent', 'ldd', 'lds', 'ldm', 'gota', 'gotb', 'acca', 'accb']
+Q = 128
+SCRATCH = {'st': ('dram', [12, 128, Q], 'float32'),
+           'in0': ('dram', [4, 128, Q], 'float32'),
+           'in1': ('dram', [4, 128, Q], 'float32')}
+SEMAPHORES = ['y0', 'sent', 'ldd', 'lds', 'ldm', 'gota', 'gotb', 'gotr', 'acca', 'accb']
 
 
 def rank_program(g, core, T, topo):
@@ -23,38 +21,59 @@ def rank_program(g, core, T, topo):
         return RemoteDMATransfer(dst_ids=[DstId(rid=rid, pnc=pid)], dma_engine_mask=mask, remote_sem=rsem,
                                  srcs=srcs, dsts=[out], alu_op=1 if len(srcs) > 1 else 0)
 
+    def send(*trs):
+        g.remote_dma_fused(list(trs), local_sem=S.sent)
+
     if k == 0:
         def blk(t):
             return T.x[32 * t:32 * t + 32, :]
-        g.sync.dma_start(T.st[0:2], blk(r ^ 3)).then_inc(S.ldd, 16)
-        g.scalar.dma_start(T.st[2:4], blk(r ^ 2)).then_inc(S.lds, 16)
-        g.sync.dma_start(T.st[4:6], blk(r ^ 1)).then_inc(S.ldm, 16)
+        g.sync.dma_start(T.st[0:4], blk(r ^ 3)).then_inc(S.ldd, 16)
+        g.scalar.dma_start(T.st[4:8], blk(r ^ 2)).then_inc(S.lds, 16)
+        g.sync.dma_start(T.st[8:12], blk(r ^ 1)).then_inc(S.ldm, 16)
         g.scalar.dma_start(T.y[:, :], blk(r)).then_inc(S.y0, 16)
         g.wait_ge(S.ldd, 16)
-        g.remote_dma_fused([tr(peer + f, [T.st[i]], T.in1[i], 15 << 4 * i, S.gotb)
-                            for i, f in enumerate(FOLD)], local_sem=S.sent)
+        send(tr(peer + 2, [T.st[0]], T.in1[0], 0x000F, S.gotb),
+             tr(peer + 6, [T.st[1]], T.in1[1], 0x00F0, S.gotb),
+             tr(home + 3, [T.st[2]], T.in0[2], 0x0F00, S.gota),
+             tr(home + 7, [T.st[3]], T.in0[3], 0xF000, S.gota))
         g.wait_ge(S.lds, 16)
-        g.remote_dma_fused([tr(home + f, [T.st[2 + i]], T.in0[i], 15 << 8 + 4 * i, S.gota)
-                            for i, f in enumerate(RELAY)], local_sem=S.sent)
+        send(tr(home + 4, [T.st[4]], T.in0[0], 0x0F00, S.gota),
+             tr(home + 4, [T.st[5]], T.in0[1], 0xF000, S.gota),
+             tr(home + 1, [T.st[6]], T.in0[2], 0x000F, S.gota),
+             tr(home + 5, [T.st[7]], T.in0[3], 0x00F0, S.gota))
         g.wait_ge(S.ldm, 16)
-        g.remote_dma_fused([tr(home + f, [T.st[4 + i]], T.in0[i], 15 << 8 + 4 * i, S.gota)
-                            for i, f in enumerate(FOLD)], local_sem=S.sent)
+        send(tr(home + 2, [T.st[10]], T.in0[2], 0x0F00, S.gotr),
+             tr(home + 6, [T.st[11]], T.in0[3], 0xF000, S.gotr),
+             tr(home + 2, [T.st[8]], T.in0[0], 0x000F, S.gota),
+             tr(home + 6, [T.st[9]], T.in0[1], 0x00F0, S.gota))
         g.wait_ge(S.y0, 16)
-        g.wait_ge(S.gota, 16)
+        g.wait_ge(S.gota, 24)
         g.dma_start(out=T.y[:, :], in_=T.in0[:], accum_op=AluOpType.add, max_dma_last_dim=8192).then_inc(S.acca, 16)
         g.wait_ge(S.acca, 16)
-        g.wait_ge(S.gotb, 16)
+        g.wait_ge(S.gotb, 32)
         g.dma_start(out=T.y[:, :], in_=T.in1[:], accum_op=AluOpType.add, max_dma_last_dim=8192).then_inc(S.accb, 16)
         g.wait_ge(S.accb, 16)
-        g.wait_ge(S.sent, 24)
-    elif k in FOLD:
-        i = FOLD.index(k)
+        g.wait_ge(S.sent, 48)
+    elif k in (2, 6):
+        i = 0 if k == 2 else 1
+        g.wait_ge(S.gotr, 4)
+        send(tr(mate, [T.in0[2 + i]], T.in0[2 + i], 255, S.gota))
         g.wait_ge(S.gota, 4)
         g.wait_ge(S.gotb, 4)
-        g.remote_dma_fused([tr(mate, [T.in0[i], T.in1[i]], T.in1[i], 255, S.gotb)], local_sem=S.sent)
-        g.wait_ge(S.sent, 8)
-    elif k in RELAY:
-        i = RELAY.index(k)
+        send(tr(mate, [T.in0[i], T.in1[i]], T.in1[i], 255, S.gotb))
+        g.wait_ge(S.sent, 16)
+    elif k in (3, 7):
+        q = 2 if k == 3 else 3
         g.wait_ge(S.gota, 4)
-        g.remote_dma_fused([tr(peer, [T.in0[i]], T.in0[i], 255, S.gota)], local_sem=S.sent)
+        send(tr(mate + (1 if k == 3 else 5), [T.in0[q]], T.in1[q], 255, S.gotb))
+        g.wait_ge(S.sent, 8)
+    elif k in (1, 5):
+        q = 2 if k == 1 else 3
+        g.wait_ge(S.gota, 4)
+        g.wait_ge(S.gotb, 8)
+        send(tr(peer, [T.in0[q], T.in1[q]], T.in1[q], 255, S.gotb))
+        g.wait_ge(S.sent, 8)
+    elif k == 4:
+        g.wait_ge(S.gota, 8)
+        send(tr(peer, [T.in0[0]], T.in0[0], 0x0F, S.gota), tr(peer, [T.in0[1]], T.in0[1], 0xF0, S.gota))
         g.wait_ge(S.sent, 8)

@@ -25,25 +25,31 @@ def rank_program(g, core, T, topo):
         g.remote_dma_fused(list(trs), local_sem=S.sent)
 
     if k == 0:
-        def blk(t):
-            return T.x[32 * t:32 * t + 32, :]
+        def blk(t, h=None):
+            if h is None:
+                return T.x[32 * t:32 * t + 32, :]
+            return T.x[32 * t + 16 * h:32 * t + 16 * h + 16, :]
         g.sync.dma_start(T.st[0:4], blk(r ^ 3)).then_inc(S.ldd, 16)
-        g.scalar.dma_start(T.st[4:8], blk(r ^ 2)).then_inc(S.lds, 16)
-        g.sync.dma_start(T.st[8:12], blk(r ^ 1)).then_inc(S.ldm, 16)
+        g.scalar.dma_start(T.st[4:6], blk(r ^ 2, 0)).then_inc(S.lds, 16)
+        g.scalar.dma_start(T.st[10:12], blk(r ^ 1, 1)).then_inc(S.lds, 16)
+        g.sync.wait_ge(S.ldd, 16)
+        g.sync.dma_start(T.st[6:8], blk(r ^ 2, 1)).then_inc(S.ldm, 16)
+        g.sync.dma_start(T.st[8:10], blk(r ^ 1, 0)).then_inc(S.ldm, 16)
+        g.scalar.wait_ge(S.ldm, 32)
         g.scalar.dma_start(T.y[:, :], blk(r)).then_inc(S.y0, 16)
         g.wait_ge(S.ldd, 16)
         send(tr(peer + 2, [T.st[0]], T.in1[0], 0x000F, S.gotb),
              tr(peer + 6, [T.st[1]], T.in1[1], 0x00F0, S.gotb),
              tr(home + 3, [T.st[2]], T.in0[2], 0x0F00, S.gota),
              tr(home + 7, [T.st[3]], T.in0[3], 0xF000, S.gota))
-        g.wait_ge(S.lds, 16)
+        g.wait_ge(S.lds, 32)
         send(tr(home + 4, [T.st[4]], T.in0[0], 0x0F00, S.gota),
              tr(home + 4, [T.st[5]], T.in0[1], 0xF000, S.gota),
-             tr(home + 1, [T.st[6]], T.in0[2], 0x000F, S.gota),
-             tr(home + 5, [T.st[7]], T.in0[3], 0x00F0, S.gota))
-        g.wait_ge(S.ldm, 16)
-        send(tr(home + 2, [T.st[10]], T.in0[2], 0x0F00, S.gotr),
-             tr(home + 6, [T.st[11]], T.in0[3], 0xF000, S.gotr),
+             tr(home + 2, [T.st[10]], T.in0[2], 0x000F, S.gotr),
+             tr(home + 6, [T.st[11]], T.in0[3], 0x00F0, S.gotr))
+        g.wait_ge(S.ldm, 32)
+        send(tr(home + 1, [T.st[6]], T.in0[2], 0x0F00, S.gota),
+             tr(home + 5, [T.st[7]], T.in0[3], 0xF000, S.gota),
              tr(home + 2, [T.st[8]], T.in0[0], 0x000F, S.gota),
              tr(home + 6, [T.st[9]], T.in0[1], 0x00F0, S.gota))
         g.wait_ge(S.y0, 16)

@@ -1,11 +1,14 @@
 from concourse.bass import DstId, RemoteDMATransfer
-from concourse.mybir import AluOpType
 
 Q = 128
-SCRATCH = {'st': ('dram', [12, 128, Q], 'float32'),
+HC = (3, 7, 1, 4)
+SCRATCH = {'st': ('dram', [16, 128, Q], 'float32'),
            'in0': ('dram', [4, 128, Q], 'float32'),
-           'in1': ('dram', [4, 128, Q], 'float32')}
-SEMAPHORES = ['y0', 'sent', 'ldd', 'lds', 'ldm', 'gota', 'gotb', 'gotr', 'acca', 'accb']
+           'in1': ('dram', [4, 128, Q], 'float32'),
+           'h0': ('dram', [128, Q], 'float32'),
+           'h1': ('dram', [128, Q], 'float32'),
+           'h2': ('dram', [128, Q], 'float32')}
+SEMAPHORES = ['y0', 'sent', 'ldd', 'lds', 'ldm', 'ldo', 'gota', 'gotb', 'gotr', 'goth']
 
 
 def rank_program(g, core, T, topo):
@@ -24,6 +27,10 @@ def rank_program(g, core, T, topo):
     def send(*trs):
         g.remote_dma_fused(list(trs), local_sem=S.sent)
 
+    def last(n):
+        g.wait_ge(S.goth, n)
+        send(tr(home, [T.h0[:, :], T.h1[:, :], T.h2[:, :]], T.in1[HC.index(k)], 0xFFFF, S.gotb))
+
     if k == 0:
         def blk(t, h=None):
             if h is None:
@@ -36,7 +43,7 @@ def rank_program(g, core, T, topo):
         g.sync.dma_start(T.st[6:8], blk(r ^ 2, 1)).then_inc(S.ldm, 16)
         g.sync.dma_start(T.st[8:10], blk(r ^ 1, 0)).then_inc(S.ldm, 16)
         g.scalar.wait_ge(S.ldm, 32)
-        g.scalar.dma_start(T.y[:, :], blk(r)).then_inc(S.y0, 16)
+        g.scalar.dma_start(T.st[12:16], blk(r)).then_inc(S.ldo, 16)
         g.wait_ge(S.ldd, 16)
         send(tr(peer + 2, [T.st[0]], T.in1[0], 0x000F, S.gotb),
              tr(peer + 6, [T.st[1]], T.in1[1], 0x00F0, S.gotb),
@@ -52,34 +59,38 @@ def rank_program(g, core, T, topo):
              tr(home + 5, [T.st[7]], T.in0[3], 0xF000, S.gota),
              tr(home + 2, [T.st[8]], T.in0[0], 0x000F, S.gota),
              tr(home + 6, [T.st[9]], T.in0[1], 0x00F0, S.gota))
+        g.wait_ge(S.ldo, 16)
+        send(*[tr(home + HC[q], [T.st[12 + q]], T.h0[:, :], 15 << 4 * q, S.goth) for q in range(4)])
+        g.sync.wait_ge(S.gotb, 64)
+        g.sync.dma_start(T.y[:, :], T.in1[:]).then_inc(S.y0, 16)
+        g.wait_ge(S.sent, 64)
         g.wait_ge(S.y0, 16)
-        g.wait_ge(S.gota, 24)
-        g.dma_start(out=T.y[:, :], in_=T.in0[:], accum_op=AluOpType.add, max_dma_last_dim=8192).then_inc(S.acca, 16)
-        g.wait_ge(S.acca, 16)
-        g.wait_ge(S.gotb, 32)
-        g.dma_start(out=T.y[:, :], in_=T.in1[:], accum_op=AluOpType.add, max_dma_last_dim=8192).then_inc(S.accb, 16)
-        g.wait_ge(S.accb, 16)
-        g.wait_ge(S.sent, 48)
     elif k in (2, 6):
         i = 0 if k == 2 else 1
         g.wait_ge(S.gotr, 4)
-        send(tr(mate, [T.in0[2 + i]], T.in0[2 + i], 255, S.gota))
+        send(tr(mate + HC[2 + i], [T.in0[2 + i]], T.h1[:, :], 255, S.goth))
         g.wait_ge(S.gota, 4)
         g.wait_ge(S.gotb, 4)
-        send(tr(mate, [T.in0[i], T.in1[i]], T.in1[i], 255, S.gotb))
+        send(tr(mate + HC[i], [T.in0[i], T.in1[i]], T.h2[:, :], 255, S.goth))
         g.wait_ge(S.sent, 16)
     elif k in (3, 7):
         q = 2 if k == 3 else 3
         g.wait_ge(S.gota, 4)
         send(tr(mate + (1 if k == 3 else 5), [T.in0[q]], T.in1[q], 255, S.gotb))
-        g.wait_ge(S.sent, 8)
+        last(16)
+        g.wait_ge(S.sent, 24)
     elif k in (1, 5):
         q = 2 if k == 1 else 3
         g.wait_ge(S.gota, 4)
         g.wait_ge(S.gotb, 8)
-        send(tr(peer, [T.in0[q], T.in1[q]], T.in1[q], 255, S.gotb))
-        g.wait_ge(S.sent, 8)
+        send(tr(peer + HC[q], [T.in0[q], T.in1[q]], T.h2[:, :], 255, S.goth))
+        if k == 1:
+            last(20)
+            g.wait_ge(S.sent, 24)
+        else:
+            g.wait_ge(S.sent, 8)
     elif k == 4:
         g.wait_ge(S.gota, 8)
-        send(tr(peer, [T.in0[0]], T.in0[0], 0x0F, S.gota), tr(peer, [T.in0[1]], T.in0[1], 0xF0, S.gota))
-        g.wait_ge(S.sent, 8)
+        send(tr(peer + HC[0], [T.in0[0]], T.h1[:, :], 0x0F, S.goth), tr(peer + HC[1], [T.in0[1]], T.h1[:, :], 0xF0, S.goth))
+        last(20)
+        g.wait_ge(S.sent, 24)

@@ -8,7 +8,7 @@ SCRATCH = {'st': ('dram', [16, 128, Q], 'float32'),
            'h0': ('dram', [128, Q], 'float32'),
            'h1': ('dram', [128, Q], 'float32'),
            'h2': ('dram', [128, Q], 'float32')}
-SEMAPHORES = ['y0', 'sent', 'ldd', 'lds', 'ldm', 'ldo', 'gota', 'gotb', 'gotr', 'goth']
+SEMAPHORES = ['y0', 'sent', 'ldd', 'lds', 'ldm', 'ldo', 'gota', 'gotr', 'goth', 'res0', 'res1', 'res2', 'res3']
 
 
 def rank_program(g, core, T, topo):
@@ -18,6 +18,7 @@ def rank_program(g, core, T, topo):
         return
     home, mate, peer = (T.cores[r], T.cores[r ^ 1], T.cores[r ^ 2])
     S = T.sem
+    res = [S.res0, S.res1, S.res2, S.res3]
 
     def tr(dst, srcs, out, mask, rsem):
         rid, pid = topo.addr(dst, core)
@@ -28,8 +29,9 @@ def rank_program(g, core, T, topo):
         g.remote_dma_fused(list(trs), local_sem=S.sent)
 
     def last(n):
+        q = HC.index(k)
         g.wait_ge(S.goth, n)
-        send(tr(home, [T.h0[:, :], T.h1[:, :], T.h2[:, :]], T.in1[HC.index(k)], 0xFFFF, S.gotb))
+        send(tr(home, [T.h0[:, :], T.h1[:, :], T.h2[:, :]], T.in1[q], 0xFFFF, res[q]))
 
     if k == 0:
         def blk(t, h=None):
@@ -45,8 +47,8 @@ def rank_program(g, core, T, topo):
         g.scalar.wait_ge(S.ldm, 32)
         g.scalar.dma_start(T.st[12:16], blk(r)).then_inc(S.ldo, 16)
         g.wait_ge(S.ldd, 16)
-        send(tr(peer + 2, [T.st[0]], T.in1[0], 0x000F, S.gotb),
-             tr(peer + 6, [T.st[1]], T.in1[1], 0x00F0, S.gotb),
+        send(tr(peer + 2, [T.st[0]], T.in1[0], 0x000F, S.gota),
+             tr(peer + 6, [T.st[1]], T.in1[1], 0x00F0, S.gota),
              tr(home + 3, [T.st[2]], T.in0[2], 0x0F00, S.gota),
              tr(home + 7, [T.st[3]], T.in0[3], 0xF000, S.gota))
         g.wait_ge(S.lds, 32)
@@ -61,28 +63,27 @@ def rank_program(g, core, T, topo):
              tr(home + 6, [T.st[9]], T.in0[1], 0x00F0, S.gota))
         g.wait_ge(S.ldo, 16)
         send(*[tr(home + HC[q], [T.st[12 + q]], T.h0[:, :], 15 << 4 * q, S.goth) for q in range(4)])
-        g.sync.wait_ge(S.gotb, 64)
-        g.sync.dma_start(T.y[:, :], T.in1[:]).then_inc(S.y0, 16)
+        for q, eng in ((0, g.sync), (2, g.scalar), (1, g.sync), (3, g.scalar)):
+            eng.wait_ge(res[q], 16)
+            eng.dma_start(T.y[8 * q:8 * q + 8, :], T.in1[q]).then_inc(S.y0, 16)
         g.wait_ge(S.sent, 64)
-        g.wait_ge(S.y0, 16)
+        g.wait_ge(S.y0, 64)
     elif k in (2, 6):
         i = 0 if k == 2 else 1
         g.wait_ge(S.gotr, 4)
         send(tr(mate + HC[2 + i], [T.in0[2 + i]], T.h1[:, :], 255, S.goth))
-        g.wait_ge(S.gota, 4)
-        g.wait_ge(S.gotb, 4)
+        g.wait_ge(S.gota, 8)
         send(tr(mate + HC[i], [T.in0[i], T.in1[i]], T.h2[:, :], 255, S.goth))
         g.wait_ge(S.sent, 16)
     elif k in (3, 7):
         q = 2 if k == 3 else 3
         g.wait_ge(S.gota, 4)
-        send(tr(mate + (1 if k == 3 else 5), [T.in0[q]], T.in1[q], 255, S.gotb))
+        send(tr(mate + (1 if k == 3 else 5), [T.in0[q]], T.in1[q], 255, S.gota))
         last(16)
         g.wait_ge(S.sent, 24)
     elif k in (1, 5):
         q = 2 if k == 1 else 3
-        g.wait_ge(S.gota, 4)
-        g.wait_ge(S.gotb, 8)
+        g.wait_ge(S.gota, 12)
         send(tr(peer + HC[q], [T.in0[q], T.in1[q]], T.h2[:, :], 255, S.goth))
         if k == 1:
             last(20)

@@ -8,7 +8,7 @@ SCRATCH = {'st': ('dram', [16, 128, Q], 'float32'),
            'h0': ('dram', [128, Q], 'float32'),
            'h1': ('dram', [128, Q], 'float32'),
            'h2': ('dram', [128, Q], 'float32')}
-SEMAPHORES = ['y0', 'sent', 'ldd', 'lds', 'ldm', 'ldo', 'gota', 'gotr', 'goth', 'res0', 'res1', 'res2', 'res3']
+SEMAPHORES = ['y0', 'sent', 'ldd', 'lda', 'lds', 'ldm', 'ldo', 'gota', 'gotr', 'goth', 'res0', 'res1', 'res2', 'res3']
 
 
 def rank_program(g, core, T, topo):
@@ -38,7 +38,8 @@ def rank_program(g, core, T, topo):
             if h is None:
                 return T.x[32 * t:32 * t + 32, :]
             return T.x[32 * t + 16 * h:32 * t + 16 * h + 16, :]
-        g.sync.dma_start(T.st[0:4], blk(r ^ 3)).then_inc(S.ldd, 16)
+        g.sync.dma_start(T.st[2:4], blk(r ^ 3, 1)).then_inc(S.ldd, 16)
+        g.scalar.dma_start(T.st[0:2], blk(r ^ 3, 0)).then_inc(S.lda, 16)
         g.scalar.dma_start(T.st[4:6], blk(r ^ 2, 0)).then_inc(S.lds, 16)
         g.scalar.dma_start(T.st[10:12], blk(r ^ 1, 1)).then_inc(S.lds, 16)
         g.sync.wait_ge(S.ldd, 16)
@@ -47,10 +48,11 @@ def rank_program(g, core, T, topo):
         g.scalar.wait_ge(S.ldm, 32)
         g.scalar.dma_start(T.st[12:16], blk(r)).then_inc(S.ldo, 16)
         g.wait_ge(S.ldd, 16)
+        send(tr(home + 3, [T.st[2]], T.in0[2], 0xFF00, S.gota),
+             tr(home + 7, [T.st[3]], T.in0[3], 0x00FF, S.gota))
+        g.wait_ge(S.lda, 16)
         send(tr(peer + 2, [T.st[0]], T.in1[0], 0x000F, S.gota),
-             tr(peer + 6, [T.st[1]], T.in1[1], 0x00F0, S.gota),
-             tr(home + 3, [T.st[2]], T.in0[2], 0x0F00, S.gota),
-             tr(home + 7, [T.st[3]], T.in0[3], 0xF000, S.gota))
+             tr(peer + 6, [T.st[1]], T.in1[1], 0x00F0, S.gota))
         g.wait_ge(S.lds, 32)
         send(tr(home + 4, [T.st[4]], T.in0[0], 0x0F00, S.gota),
              tr(home + 4, [T.st[5]], T.in0[1], 0xF000, S.gota),
@@ -66,7 +68,7 @@ def rank_program(g, core, T, topo):
         for q, eng in ((0, g.sync), (2, g.scalar), (1, g.sync), (3, g.scalar)):
             eng.wait_ge(res[q], 16)
             eng.dma_start(T.y[8 * q:8 * q + 8, :], T.in1[q]).then_inc(S.y0, 16)
-        g.wait_ge(S.sent, 64)
+        g.wait_ge(S.sent, 72)
         g.wait_ge(S.y0, 64)
     elif k in (2, 6):
         i = 0 if k == 2 else 1
@@ -77,7 +79,7 @@ def rank_program(g, core, T, topo):
         g.wait_ge(S.sent, 16)
     elif k in (3, 7):
         q = 2 if k == 3 else 3
-        g.wait_ge(S.gota, 4)
+        g.wait_ge(S.gota, 8)
         send(tr(mate + (1 if k == 3 else 5), [T.in0[q]], T.in1[q], 255, S.gota))
         last(16)
         g.wait_ge(S.sent, 24)

from concourse.bass import DstId, RemoteDMATransfer

Q = 128
HC = (3, 7, 1, 4)
SCRATCH = {'st': ('dram', [16, 128, Q], 'float32'),
           'in0': ('dram', [4, 128, Q], 'float32'),
           'in1': ('dram', [4, 128, Q], 'float32'),
           'h0': ('dram', [128, Q], 'float32'),
           'h1': ('dram', [128, Q], 'float32'),
           'h2': ('dram', [128, Q], 'float32')}
SEMAPHORES = ['y0', 'sent', 'ldd', 'lda', 'lds', 'ldm', 'ldo', 'gota', 'gotr', 'goth', 'res0', 'res1', 'res2', 'res3']


def rank_program(g, core, T, topo):
    k = core % 8
    r = T.rank_of(core - k)
    if r is None:
        return
    home, mate, peer = (T.cores[r], T.cores[r ^ 1], T.cores[r ^ 2])
    S = T.sem
    res = [S.res0, S.res1, S.res2, S.res3]

    def tr(dst, srcs, out, mask, rsem):
        rid, pid = topo.addr(dst, core)
        return RemoteDMATransfer(dst_ids=[DstId(rid=rid, pnc=pid)], dma_engine_mask=mask, remote_sem=rsem,
                                 srcs=srcs, dsts=[out], alu_op=1 if len(srcs) > 1 else 0)

    def send(*trs):
        g.remote_dma_fused(list(trs), local_sem=S.sent)

    def last(n):
        q = HC.index(k)
        g.wait_ge(S.goth, n)
        send(tr(home, [T.h0[:, :], T.h1[:, :], T.h2[:, :]], T.in1[q], 0xFFFF, res[q]))

    if k == 0:
        def blk(t, h=None):
            if h is None:
                return T.x[32 * t:32 * t + 32, :]
            return T.x[32 * t + 16 * h:32 * t + 16 * h + 16, :]
        g.sync.dma_start(T.st[2:4], blk(r ^ 3, 1)).then_inc(S.ldd, 16)
        g.scalar.dma_start(T.st[0:2], blk(r ^ 3, 0)).then_inc(S.lda, 16)
        g.scalar.dma_start(T.st[4:6], blk(r ^ 2, 0)).then_inc(S.lds, 16)
        g.scalar.dma_start(T.st[10:12], blk(r ^ 1, 1)).then_inc(S.lds, 16)
        g.sync.wait_ge(S.ldd, 16)
        g.sync.dma_start(T.st[6:8], blk(r ^ 2, 1)).then_inc(S.ldm, 16)
        g.sync.dma_start(T.st[8:10], blk(r ^ 1, 0)).then_inc(S.ldm, 16)
        g.scalar.wait_ge(S.ldm, 32)
        g.scalar.dma_start(T.st[12:16], blk(r)).then_inc(S.ldo, 16)
        g.wait_ge(S.ldd, 16)
        send(tr(home + 3, [T.st[2]], T.in0[2], 0xFF00, S.gota),
             tr(home + 7, [T.st[3]], T.in0[3], 0x00FF, S.gota))
        g.wait_ge(S.lda, 16)
        send(tr(peer + 2, [T.st[0]], T.in1[0], 0x000F, S.gota),
             tr(peer + 6, [T.st[1]], T.in1[1], 0x00F0, S.gota))
        g.wait_ge(S.lds, 32)
        send(tr(home + 4, [T.st[4]], T.in0[0], 0x0F00, S.gota),
             tr(home + 4, [T.st[5]], T.in0[1], 0xF000, S.gota),
             tr(home + 2, [T.st[10]], T.in0[2], 0x000F, S.gotr),
             tr(home + 6, [T.st[11]], T.in0[3], 0x00F0, S.gotr))
        g.wait_ge(S.ldm, 32)
        send(tr(home + 1, [T.st[6]], T.in0[2], 0x0F00, S.gota),
             tr(home + 5, [T.st[7]], T.in0[3], 0xF000, S.gota),
             tr(home + 2, [T.st[8]], T.in0[0], 0x000F, S.gota),
             tr(home + 6, [T.st[9]], T.in0[1], 0x00F0, S.gota))
        g.wait_ge(S.ldo, 16)
        send(*[tr(home + HC[q], [T.st[12 + q]], T.h0[:, :], 15 << 4 * q, S.goth) for q in range(4)])
        for q, eng in ((0, g.sync), (2, g.scalar), (1, g.sync), (3, g.scalar)):
            eng.wait_ge(res[q], 16)
            eng.dma_start(T.y[8 * q:8 * q + 8, :], T.in1[q]).then_inc(S.y0, 16)
        g.wait_ge(S.sent, 72)
        g.wait_ge(S.y0, 64)
    elif k in (2, 6):
        i = 0 if k == 2 else 1
        g.wait_ge(S.gotr, 4)
        send(tr(mate + HC[2 + i], [T.in0[2 + i]], T.h1[:, :], 255, S.goth))
        g.wait_ge(S.gota, 8)
        send(tr(mate + HC[i], [T.in0[i], T.in1[i]], T.h2[:, :], 255, S.goth))
        g.wait_ge(S.sent, 16)
    elif k in (3, 7):
        q = 2 if k == 3 else 3
        g.wait_ge(S.gota, 8)
        send(tr(mate + (1 if k == 3 else 5), [T.in0[q]], T.in1[q], 255, S.gota))
        last(16)
        g.wait_ge(S.sent, 24)
    elif k in (1, 5):
        q = 2 if k == 1 else 3
        g.wait_ge(S.gota, 12)
        send(tr(peer + HC[q], [T.in0[q], T.in1[q]], T.h2[:, :], 255, S.goth))
        if k == 1:
            last(20)
            g.wait_ge(S.sent, 24)
        else:
            g.wait_ge(S.sent, 8)
    elif k == 4:
        g.wait_ge(S.gota, 8)
        send(tr(peer + HC[0], [T.in0[0]], T.h1[:, :], 0x0F, S.goth), tr(peer + HC[1], [T.in0[1]], T.h1[:, :], 0xF0, S.goth))
        last(20)
        g.wait_ge(S.sent, 24)
